import numpy as np
import ml_dtypes


def mxq(x, axis, fmt="e4m3"):
    dtype, down = {"e4m3": (ml_dtypes.float8_e4m3fn, 7), "e5m2": (ml_dtypes.float8_e5m2, 14)}[fmt]
    v = np.moveaxis(np.asarray(x, np.float32).astype(ml_dtypes.bfloat16).astype(np.float64), axis, -1)
    blocks = v.reshape(v.shape[:-1] + (-1, 32))
    amax = np.abs(blocks).max(-1, keepdims=True)
    byte = np.maximum(np.where(amax > 0, np.frexp(amax)[1] - 1 + 127, 0) - down, 1)
    scale = np.exp2(byte - 127.0)
    codes = (blocks / scale).astype(np.float32).astype(dtype).astype(np.float64)
    return np.moveaxis((codes * scale).reshape(v.shape), -1, axis)


WIDE = False


def mx_kscale(k, group=512):
    if not WIDE:
        return np.ones(k)
    levels = np.array([10, -10, 5, -5, 0])
    if group != 512:
        return np.exp2(np.random.permutation(np.resize(levels, k // group))).repeat(group)
    if k % 512:
        return np.exp2(np.random.permutation(np.resize(levels, k // 32))).repeat(32)
    a = np.empty((k // 512, 16))
    for p in range(k // 512):
        a[p, :8] = np.random.permutation(np.resize(levels, 8))
        for g in range(8):
            far = levels[np.abs(levels - a[p, g]) >= 10]
            a[p, g + 8] = far[np.random.randint(len(far))]
    return np.exp2(a.ravel()).repeat(32)


def f64(x):
    return np.asarray(x).astype(np.float64)


def striped(idx):
    return np.tile(np.asarray(idx).reshape(-1, 16).T, (8, 1)).astype(np.uint16)


def unstriped(offs):
    return offs[:16].T.reshape(-1).astype(np.int64)


H, KV, D, NQ, N = 2, 2, 256, 512, 512


def setup_inputs():
    n = np.random.standard_normal
    s = mx_kscale(D, 0)[:, None]
    u = mx_kscale(N)
    t = np.random.uniform(0.5, 2.0, N) * u
    v = n((KV, N, 128))
    return {
        "qT": (n((H, D, NQ)) * s * (0.70 / np.sqrt(D))).astype(np.float32),
        "kT": (n((KV, D, N)) / s).astype(np.float32),
        "t": t.reshape(N, 1).astype(np.float32),
        "v": (v / t[:, None]).astype(np.float32),
        "mask": (np.arange(N)[:, None] <= np.sort(np.random.randint(N // 4, N, NQ))[None, :]).astype(np.float32),
    }


def reference(qT, kT, t, v, mask):
    a = mxq(f64(kT), 1, "e4m3").transpose(0, 2, 1) @ mxq(f64(qT), 1, "e4m3")
    p = np.tanh(a)
    p = p * f64(mask)
    w = p * f64(t)
    y = mxq(w, 1, "e4m3").transpose(0, 2, 1) @ mxq(f64(v), 1, "e4m3")
    y = y / 16.0
    return y

@@ -1,0 +1,230 @@
+from contextlib import ExitStack
+
+import concourse.mybir as mybir
+
+H, D, NQ, N, E = 2, 256, 512, 512, 128
+FLOPS = 2 * H * N * NQ * D + 2 * H * NQ * N * E
+
+F32 = mybir.dt.float32
+BF16 = mybir.dt.bfloat16
+U32 = mybir.dt.uint32
+U8 = mybir.dt.uint8
+FP8X4 = mybir.dt.float8_e4m3fn_x4
+ACT = mybir.ActivationFunctionType
+ALU = mybir.AluOpType
+
+P = 128
+ROWS = 64
+PACK = 4
+QT = 128
+TILES = NQ // QT
+
+
+def tile_rows_a_tanh_mask_kernel(tc, qT, kT, t, v, mask, out):
+    nc = tc.nc
+    with ExitStack() as ctx:
+        sb = ctx.enter_context(tc.tile_pool(name="sb", bufs=1))
+        ps = ctx.enter_context(tc.psum_pool(name="ps", bufs=1))
+        ctx.enter_context(tc.manual_schedule())
+
+        def sbt(name, shape, dtype):
+            return sb.tile(shape, dtype, name=name, align_bytes=64)
+
+        q_hbm = qT.rearrange("h (p j) n -> (h p) j n", j=PACK)
+        k_hbm = kT.rearrange("h (p j) n -> (h p) j n", j=PACK)
+        m_hbm = mask.rearrange("(p r) n -> p r n", r=PACK)
+        v_hbm = v.rearrange("h (p j) e -> p h (j e)", j=PACK)
+        t_hbm = t.rearrange("(p r) o -> p (r o)", r=PACK)
+
+        q_loads = [(0, 1), (1, 1), (2, 2)]
+        m_loads = [(0, 1), (1, 1), (2, 2)]
+        q_raw = [sbt("q_raw%d" % i, [P, PACK, n * QT], F32) for i, (a, n) in enumerate(q_loads)]
+        m_raw = [sbt("m_raw%d" % i, [P, PACK, n * QT], F32) for i, (a, n) in enumerate(m_loads)]
+        tm = [sbt("tm%d" % i, [P, PACK, n * QT], F32) for i, (a, n) in enumerate(m_loads)]
+        k_raw = sbt("k_raw", [P, PACK, N], F32)
+        v_raw = sbt("v_raw", [P, H, PACK * E], F32)
+        t_sb = sbt("t_sb", [P, PACK], F32)
+        zero_in = sbt("zero_in", [P, 1], F32)
+        zero = sbt("zero", [P, 1], F32)
+
+        q_bf = [sbt("q_bf%d" % i, [P, QT * PACK], BF16) for i in range(TILES)]
+        q_codes = [sbt("q_codes%d" % i, [P, QT], U32) for i in range(TILES)]
+        q_scales = [sbt("q_scales%d" % i, [P, QT], U8) for i in range(TILES)]
+        k_bf = [sbt("k_bf%d" % a, [P, 2 * P * PACK], BF16) for a in range(2)]
+        k_codes = [sbt("k_codes%d" % a, [P, 2 * P], U32) for a in range(2)]
+        k_scales = [sbt("k_scales%d" % a, [P, 2 * P], U8) for a in range(2)]
+        v_bf = sbt("v_bf", [P, H * E * PACK], BF16)
+        v_codes = sbt("v_codes", [P, H * E], U32)
+        v_scales = sbt("v_scales", [P, H * E], U8)
+        p_sb = [[sbt("p%d_%d" % (i, h), [P, PACK * QT], F32) for h in range(H)] for i in range(TILES)]
+        w_bf = [sbt("w_bf%d" % i, [P, H * QT * PACK], BF16) for i in range(TILES)]
+        w_codes = [sbt("w_codes%d" % i, [P, H * QT], U32) for i in range(TILES)]
+        w_scales = [sbt("w_scales%d" % i, [P, H * QT], U8) for i in range(TILES)]
+        y_sb = [[sbt("y%d_%d" % (h, b), [P, n * E], F32) for b, n in enumerate((3, 1))] for h in range(H)]
+
+        s_ps = [[ps.tile([P, PACK * QT], F32, name="s%d_%d" % (h, b)) for b in range(2)] for h in range(H)]
+        y_ps = [[ps.tile([P, PACK * E], F32, name="yp%d_%d" % (h, b)) for b in range(2)] for h in range(H)]
+
+        def find(loads, i):
+            for n_load, (a, n) in enumerate(loads):
+                if a <= i < a + n:
+                    return n_load, slice((i - a) * QT, (i - a + 1) * QT)
+            raise ValueError("no load")
+
+        def load_q(n_load):
+            a, n = q_loads[n_load]
+            nc.sync.dma_start(out=q_raw[n_load][:], in_=q_hbm[:, :, a * QT:(a + n) * QT])
+
+        def load_m(n_load):
+            a, n = m_loads[n_load]
+            nc.sync.dma_start(out=m_raw[n_load][:], in_=m_hbm[:, :, a * QT:(a + n) * QT])
+
+        def cast(on_vector, dst, src):
+            if on_vector:
+                nc.vector.tensor_copy(out=dst, in_=src)
+            else:
+                nc.scalar.copy(out=dst, in_=src)
+
+        def cast_q(i, on_vector):
+            n_load, cols = find(q_loads, i)
+            cast(on_vector,
+                 q_bf[i][:].rearrange("p (c i j) -> p c j i", i=2, j=PACK),
+                 q_raw[n_load][:, :, cols].rearrange("p j (c i) -> p c j i", i=2))
+
+        def cast_k(a, on_vector):
+            cast(on_vector,
+                 k_bf[a][:].rearrange("p (r s j) -> p s j r", r=2, j=PACK),
+                 k_raw[:].rearrange("p j (s r) -> p s j r", r=PACK)[:, :, :, 2 * a:2 * a + 2])
+
+        def cast_v(h, on_vector):
+            cast(on_vector,
+                 v_bf[:, h * E * PACK:(h + 1) * E * PACK].rearrange("p (c i j) -> p c j i", i=2, j=PACK),
+                 v_raw[:, h, :].rearrange("p (j c i) -> p c j i", i=2, j=PACK))
+
+        def quant(codes, scales, src):
+            nc.vector.quantize_mx(out=codes.bitcast(FP8X4), scales=scales, in_=src)
+
+        def quant_q(i):
+            quant(q_codes[i][:], q_scales[i][:], q_bf[i][:])
+
+        def quant_w(i, heads):
+            a, b = heads[0], heads[-1] + 1
+            quant(w_codes[i][:, a * QT:b * QT], w_scales[i][:, a * QT:b * QT], w_bf[i][:, a * QT * PACK:b * QT * PACK])
+
+        def make_tm(n_load):
+            for r in range(PACK):
+                nc.vector.tensor_scalar(out=tm[n_load][:, r, :], in0=m_raw[n_load][:, r, :],
+                                        scalar1=t_sb[:, r:r + 1], scalar2=None, op0=ALU.mult)
+
+        def scores(i):
+            for r, h in ((0, 0), (0, 1), (1, 0), (1, 1), (2, 0), (3, 0), (2, 1), (3, 1)):
+                if True:
+                    rows = slice(h * ROWS, (h + 1) * ROWS)
+                    cols = slice((r % 2) * P, (r % 2 + 1) * P)
+                    nc.tensor.matmul_mx(
+                        out=s_ps[h][i % 2][:, r * QT:(r + 1) * QT],
+                        lhsT=k_codes[r // 2][rows, cols].bitcast(FP8X4),
+                        lhsT_scale=k_scales[r // 2][rows, cols],
+                        rhs=q_codes[i][rows, :].bitcast(FP8X4),
+                        rhs_scale=q_scales[i][rows, :],
+                        start=True, stop=True)
+
+        def tanh(i, h):
+            nc.scalar.activation(out=p_sb[i][h][:], in_=s_ps[h][i % 2][:], func=ACT.Tanh, bias=zero[:])
+
+        def weigh(i, h):
+            n_load, cols = find(m_loads, i)
+            nc.vector.tensor_tensor(
+                out=w_bf[i][:, h * QT * PACK:(h + 1) * QT * PACK].rearrange("p (c i r) -> p c r i", i=2, r=PACK),
+                in0=p_sb[i][h][:].rearrange("p (r c i) -> p c r i", i=2, r=PACK),
+                in1=tm[n_load][:, :, cols].rearrange("p r (c i) -> p c r i", i=2),
+                op=ALU.mult)
+
+        def product(i, h):
+            b, x = (0, i) if i < 3 else (1, 0)
+            cols = slice(h * QT, (h + 1) * QT)
+            nc.tensor.matmul_mx(
+                out=y_ps[h][b][:, x * E:(x + 1) * E],
+                lhsT=w_codes[i][:, cols].bitcast(FP8X4),
+                lhsT_scale=w_scales[i][:, cols],
+                rhs=v_codes[:, h * E:(h + 1) * E].bitcast(FP8X4),
+                rhs_scale=v_scales[:, h * E:(h + 1) * E],
+                start=True, stop=True)
+
+        def finish(h, b, on_vector):
+            n = 3 if b == 0 else 1
+            a = 0 if b == 0 else 3
+            if on_vector:
+                nc.vector.tensor_scalar(out=y_sb[h][b][:], in0=y_ps[h][b][:, :n * E], scalar1=1.0 / 16.0,
+                                        scalar2=None, op0=ALU.mult)
+            else:
+                nc.scalar.activation(out=y_sb[h][b][:], in_=y_ps[h][b][:, :n * E], func=ACT.Copy, scale=1.0 / 16.0)
+            nc.sync.dma_start(
+                out=out[h, a * QT:(a + n) * QT, :].rearrange("(x p) e -> p x e", p=QT),
+                in_=y_sb[h][b][:].rearrange("p (x e) -> p x e", e=E))
+
+        load_q(0)
+        nc.sync.dma_start(out=k_raw[:], in_=k_hbm)
+        nc.scalar.dma_start(out=t_sb[:], in_=t_hbm)
+        load_q(1)
+        load_m(0)
+        load_q(2)
+        load_m(1)
+        load_m(2)
+        nc.sync.dma_start(out=v_raw[:], in_=v_hbm)
+
+        nc.vector.memset(zero_in[:], 0.0)
+        nc.scalar.activation(out=zero[:], in_=zero_in[:], func=ACT.Tanh)
+
+        cast_q(0, True)
+        quant_q(0)
+        cast_k(0, True)
+        cast_k(1, False)
+        quant(k_codes[0][:], k_scales[0][:], k_bf[0][:])
+        quant(k_codes[1][:], k_scales[1][:], k_bf[1][:])
+        scores(0)
+        cast_q(1, False)
+        quant_q(1)
+        scores(1)
+        make_tm(0)
+        tanh(0, 0)
+        tanh(0, 1)
+        weigh(0, 0)
+        weigh(0, 1)
+        cast_q(2, False)
+        quant_q(2)
+        quant_w(0, (0, 1))
+        scores(2)
+        make_tm(1)
+        tanh(1, 0)
+        tanh(1, 1)
+        weigh(1, 0)
+        weigh(1, 1)
+        cast_q(3, False)
+        quant_q(3)
+        quant_w(1, (0, 1))
+        scores(3)
+        make_tm(2)
+        tanh(2, 0)
+        tanh(2, 1)
+        weigh(2, 0)
+        weigh(2, 1)
+        cast_v(0, False)
+        cast_v(1, False)
+        tanh(3, 0)
+        tanh(3, 1)
+        quant_w(2, (0, 1))
+        quant(v_codes[:], v_scales[:], v_bf[:])
+        for h in range(H):
+            for i in range(3):
+                product(i, h)
+        weigh(3, 0)
+        weigh(3, 1)
+        finish(0, 0, False)
+        finish(1, 0, False)
+        quant_w(3, (0,))
+        quant_w(3, (1,))
+        product(3, 0)
+        product(3, 1)
+        finish(0, 1, False)
+        finish(1, 1, True)

@@ -37,12 +37,12 @@ def tile_rows_a_tanh_mask_kernel(tc, qT, kT, t, v, mask, out):
         t_hbm = t.rearrange("(p r) o -> p (r o)", r=PACK)
 
         q_loads = [(0, 1), (1, 1), (2, 2)]
-        m_loads = [(0, 1), (1, 1), (2, 2)]
+        m_loads = [(0, 1), (1, 1), (2, 1), (3, 1)]
         q_raw = [sbt("q_raw%d" % i, [P, PACK, n * QT], F32) for i, (a, n) in enumerate(q_loads)]
         m_raw = [sbt("m_raw%d" % i, [P, PACK, n * QT], F32) for i, (a, n) in enumerate(m_loads)]
         tm = [sbt("tm%d" % i, [P, PACK, n * QT], F32) for i, (a, n) in enumerate(m_loads)]
         k_raw = sbt("k_raw", [P, PACK, N], F32)
-        v_raw = sbt("v_raw", [P, H, PACK * E], F32)
+        v_raw = [sbt("v_raw%d" % h, [P, PACK * E], F32) for h in range(H)]
         t_sb = sbt("t_sb", [P, PACK], F32)
         zero_in = sbt("zero_in", [P, 1], F32)
         zero = sbt("zero", [P, 1], F32)
@@ -53,14 +53,14 @@ def tile_rows_a_tanh_mask_kernel(tc, qT, kT, t, v, mask, out):
         k_bf = [sbt("k_bf%d" % a, [P, 2 * P * PACK], BF16) for a in range(2)]
         k_codes = [sbt("k_codes%d" % a, [P, 2 * P], U32) for a in range(2)]
         k_scales = [sbt("k_scales%d" % a, [P, 2 * P], U8) for a in range(2)]
-        v_bf = sbt("v_bf", [P, H * E * PACK], BF16)
-        v_codes = sbt("v_codes", [P, H * E], U32)
-        v_scales = sbt("v_scales", [P, H * E], U8)
+        v_bf = [sbt("v_bf%d" % h, [P, E * PACK], BF16) for h in range(H)]
+        v_codes = [sbt("v_codes%d" % h, [P, E], U32) for h in range(H)]
+        v_scales = [sbt("v_scales%d" % h, [P, E], U8) for h in range(H)]
         p_sb = [[sbt("p%d_%d" % (i, h), [P, PACK * QT], F32) for h in range(H)] for i in range(TILES)]
         w_bf = [sbt("w_bf%d" % i, [P, H * QT * PACK], BF16) for i in range(TILES)]
         w_codes = [sbt("w_codes%d" % i, [P, H * QT], U32) for i in range(TILES)]
         w_scales = [sbt("w_scales%d" % i, [P, H * QT], U8) for i in range(TILES)]
-        y_sb = [[sbt("y%d_%d" % (h, b), [P, n * E], F32) for b, n in enumerate((3, 1))] for h in range(H)]
+        y_sb = [[sbt("y%d_%d" % (h, b), [P, n * E], F32) for b, n in enumerate((2, 1, 1))] for h in range(H)]
 
         s_ps = [[ps.tile([P, PACK * QT], F32, name="s%d_%d" % (h, b)) for b in range(2)] for h in range(H)]
         y_ps = [[ps.tile([P, PACK * E], F32, name="yp%d_%d" % (h, b)) for b in range(2)] for h in range(H)]
@@ -98,8 +98,8 @@ def tile_rows_a_tanh_mask_kernel(tc, qT, kT, t, v, mask, out):
 
         def cast_v(h, on_vector):
             cast(on_vector,
-                 v_bf[:, h * E * PACK:(h + 1) * E * PACK].rearrange("p (c i j) -> p c j i", i=2, j=PACK),
-                 v_raw[:, h, :].rearrange("p (j c i) -> p c j i", i=2, j=PACK))
+                 v_bf[h][:].rearrange("p (c i j) -> p c j i", i=2, j=PACK),
+                 v_raw[h][:].rearrange("p (j c i) -> p c j i", i=2, j=PACK))
 
         def quant(codes, scales, src):
             nc.vector.quantize_mx(out=codes.bitcast(FP8X4), scales=scales, in_=src)
@@ -116,8 +116,8 @@ def tile_rows_a_tanh_mask_kernel(tc, qT, kT, t, v, mask, out):
                 nc.vector.tensor_scalar(out=tm[n_load][:, r, :], in0=m_raw[n_load][:, r, :],
                                         scalar1=t_sb[:, r:r + 1], scalar2=None, op0=ALU.mult)
 
-        def scores(i):
-            for r, h in ((0, 0), (0, 1), (1, 0), (1, 1), (2, 0), (3, 0), (2, 1), (3, 1)):
+        def scores(i, h):
+            for r in range(PACK):
                 if True:
                     rows = slice(h * ROWS, (h + 1) * ROWS)
                     cols = slice((r % 2) * P, (r % 2 + 1) * P)
@@ -141,90 +141,116 @@ def tile_rows_a_tanh_mask_kernel(tc, qT, kT, t, v, mask, out):
                 op=ALU.mult)
 
         def product(i, h):
-            b, x = (0, i) if i < 3 else (1, 0)
+            b, x = y_place[i]
             cols = slice(h * QT, (h + 1) * QT)
             nc.tensor.matmul_mx(
                 out=y_ps[h][b][:, x * E:(x + 1) * E],
                 lhsT=w_codes[i][:, cols].bitcast(FP8X4),
                 lhsT_scale=w_scales[i][:, cols],
-                rhs=v_codes[:, h * E:(h + 1) * E].bitcast(FP8X4),
-                rhs_scale=v_scales[:, h * E:(h + 1) * E],
+                rhs=v_codes[h][:].bitcast(FP8X4),
+                rhs_scale=v_scales[h][:],
                 start=True, stop=True)
 
-        def finish(h, b, on_vector):
-            n = 3 if b == 0 else 1
-            a = 0 if b == 0 else 3
+        y_place = [(0, 0), (0, 1), (1, 0), (0, 2)]
+        groups = [(0, 2), (2, 1), (3, 1)]
+
+        def load_v(h):
+            nc.sync.dma_start(out=v_raw[h][:], in_=v_hbm[:, h, :])
+
+        def quant_v(h):
+            quant(v_codes[h][:], v_scales[h][:], v_bf[h][:])
+
+        def quant_k(a):
+            quant(k_codes[a][:], k_scales[a][:], k_bf[a][:])
+
+        def finish(h, g, on_vector, queue):
+            a, n = groups[g]
+            b, x = y_place[a]
+            src = y_ps[h][b][:, x * E:(x + n) * E]
             if on_vector:
-                nc.vector.tensor_scalar(out=y_sb[h][b][:], in0=y_ps[h][b][:, :n * E], scalar1=1.0 / 16.0,
+                nc.vector.tensor_scalar(out=y_sb[h][g][:], in0=src, scalar1=1.0 / 16.0,
                                         scalar2=None, op0=ALU.mult)
             else:
-                nc.scalar.activation(out=y_sb[h][b][:], in_=y_ps[h][b][:, :n * E], func=ACT.Copy, scale=1.0 / 16.0)
-            nc.sync.dma_start(
+                nc.scalar.activation(out=y_sb[h][g][:], in_=src, func=ACT.Copy, scale=1.0 / 16.0)
+            queue.dma_start(
                 out=out[h, a * QT:(a + n) * QT, :].rearrange("(x p) e -> p x e", p=QT),
-                in_=y_sb[h][b][:].rearrange("p (x e) -> p x e", e=E))
+                in_=y_sb[h][g][:].rearrange("p (x e) -> p x e", e=E))
 
-        load_q(0)
         nc.sync.dma_start(out=k_raw[:], in_=k_hbm)
-        nc.scalar.dma_start(out=t_sb[:], in_=t_hbm)
+        nc.gpsimd.dma_start(out=t_sb[:], in_=t_hbm)
+        load_q(0)
         load_q(1)
         load_m(0)
         load_q(2)
         load_m(1)
+        load_v(0)
         load_m(2)
-        nc.sync.dma_start(out=v_raw[:], in_=v_hbm)
+        load_v(1)
+        load_m(3)
 
         nc.vector.memset(zero_in[:], 0.0)
         nc.scalar.activation(out=zero[:], in_=zero_in[:], func=ACT.Tanh)
 
-        cast_q(0, True)
-        quant_q(0)
         cast_k(0, True)
         cast_k(1, False)
-        quant(k_codes[0][:], k_scales[0][:], k_bf[0][:])
-        quant(k_codes[1][:], k_scales[1][:], k_bf[1][:])
-        scores(0)
+        cast_q(0, True)
+        quant_k(0)
+        quant_q(0)
+        quant_k(1)
+        scores(0, 0)
+        scores(0, 1)
         cast_q(1, False)
         quant_q(1)
-        scores(1)
+        scores(1, 0)
+        scores(1, 1)
         make_tm(0)
         tanh(0, 0)
         tanh(0, 1)
+        tanh(1, 0)
         weigh(0, 0)
         weigh(0, 1)
         cast_q(2, False)
-        quant_q(2)
+        cast_q(3, True)
         quant_w(0, (0, 1))
-        scores(2)
         make_tm(1)
-        tanh(1, 0)
+        quant_q(2)
+        quant_q(3)
         tanh(1, 1)
+        scores(2, 0)
+        scores(2, 1)
         weigh(1, 0)
         weigh(1, 1)
-        cast_q(3, False)
-        quant_q(3)
-        quant_w(1, (0, 1))
-        scores(3)
-        make_tm(2)
-        tanh(2, 0)
-        tanh(2, 1)
-        weigh(2, 0)
-        weigh(2, 1)
         cast_v(0, False)
+        tanh(2, 0)
+        make_tm(2)
+        quant_v(0)
+        quant_w(1, (0, 1))
+        scores(3, 0)
+        tanh(2, 1)
+        scores(3, 1)
+        weigh(2, 0)
         cast_v(1, False)
+        weigh(2, 1)
+        product(0, 0)
+        product(1, 0)
         tanh(3, 0)
-        tanh(3, 1)
+        make_tm(3)
+        quant_v(1)
         quant_w(2, (0, 1))
-        quant(v_codes[:], v_scales[:], v_bf[:])
-        for h in range(H):
-            for i in range(3):
-                product(i, h)
+        tanh(3, 1)
+        product(0, 1)
+        product(1, 1)
+        product(2, 0)
+        product(2, 1)
+        finish(0, 0, False, nc.sync)
         weigh(3, 0)
+        finish(1, 0, False, nc.sync)
         weigh(3, 1)
-        finish(0, 0, False)
-        finish(1, 0, False)
+        finish(0, 1, False, nc.sync)
+        finish(1, 1, False, nc.sync)
         quant_w(3, (0,))
         quant_w(3, (1,))
         product(3, 0)
         product(3, 1)
-        finish(0, 1, False)
-        finish(1, 1, True)
+        finish(0, 2, True, nc.sync)
+        finish(1, 2, False, nc.scalar)

@@ -47,9 +47,9 @@ def tile_rows_a_tanh_mask_kernel(tc, qT, kT, t, v, mask, out):
         zero_in = sbt("zero_in", [P, 1], F32)
         zero = sbt("zero", [P, 1], F32)
 
-        q_bf = [sbt("q_bf%d" % i, [P, QT * PACK], BF16) for i in range(TILES)]
-        q_codes = [sbt("q_codes%d" % i, [P, QT], U32) for i in range(TILES)]
-        q_scales = [sbt("q_scales%d" % i, [P, QT], U8) for i in range(TILES)]
+        q_bf = [sbt("q_bf%d" % i, [P, n * QT * PACK], BF16) for i, (a, n) in enumerate(q_loads)]
+        q_codes = [sbt("q_codes%d" % i, [P, n * QT], U32) for i, (a, n) in enumerate(q_loads)]
+        q_scales = [sbt("q_scales%d" % i, [P, n * QT], U8) for i, (a, n) in enumerate(q_loads)]
         k_bf = [sbt("k_bf%d" % a, [P, 2 * P * PACK], BF16) for a in range(2)]
         k_codes = [sbt("k_codes%d" % a, [P, 2 * P], U32) for a in range(2)]
         k_scales = [sbt("k_scales%d" % a, [P, 2 * P], U8) for a in range(2)]
@@ -65,10 +65,10 @@ def tile_rows_a_tanh_mask_kernel(tc, qT, kT, t, v, mask, out):
         s_ps = [[ps.tile([P, PACK * QT], F32, name="s%d_%d" % (h, b)) for b in range(2)] for h in range(H)]
         y_ps = [[ps.tile([P, PACK * E], F32, name="yp%d_%d" % (h, b)) for b in range(2)] for h in range(H)]
 
-        def find(loads, i):
+        def find(loads, i, count=1):
             for n_load, (a, n) in enumerate(loads):
                 if a <= i < a + n:
-                    return n_load, slice((i - a) * QT, (i - a + 1) * QT)
+                    return n_load, slice((i - a) * QT, (i - a + count) * QT)
             raise ValueError("no load")
 
         def load_q(n_load):
@@ -85,10 +85,10 @@ def tile_rows_a_tanh_mask_kernel(tc, qT, kT, t, v, mask, out):
             else:
                 nc.scalar.copy(out=dst, in_=src)
 
-        def cast_q(i, on_vector):
-            n_load, cols = find(q_loads, i)
+        def cast_q(i, on_vector, count=1):
+            n_load, cols = find(q_loads, i, count)
             cast(on_vector,
-                 q_bf[i][:].rearrange("p (c i j) -> p c j i", i=2, j=PACK),
+                 q_bf[n_load][:, cols.start * PACK:cols.stop * PACK].rearrange("p (c i j) -> p c j i", i=2, j=PACK),
                  q_raw[n_load][:, :, cols].rearrange("p j (c i) -> p c j i", i=2))
 
         def cast_k(a, on_vector):
@@ -104,19 +104,26 @@ def tile_rows_a_tanh_mask_kernel(tc, qT, kT, t, v, mask, out):
         def quant(codes, scales, src):
             nc.vector.quantize_mx(out=codes.bitcast(FP8X4), scales=scales, in_=src)
 
-        def quant_q(i):
-            quant(q_codes[i][:], q_scales[i][:], q_bf[i][:])
+        def quant_q(i, count=1):
+            n_load, cols = find(q_loads, i, count)
+            quant(q_codes[n_load][:, cols], q_scales[n_load][:, cols], q_bf[n_load][:, cols.start * PACK:cols.stop * PACK])
 
         def quant_w(i, heads):
             a, b = heads[0], heads[-1] + 1
             quant(w_codes[i][:, a * QT:b * QT], w_scales[i][:, a * QT:b * QT], w_bf[i][:, a * QT * PACK:b * QT * PACK])
 
-        def make_tm(n_load):
+        def make_tm(i, on_vector, count=1):
+            n_load, cols = find(m_loads, i, count)
             for r in range(PACK):
-                nc.vector.tensor_scalar(out=tm[n_load][:, r, :], in0=m_raw[n_load][:, r, :],
-                                        scalar1=t_sb[:, r:r + 1], scalar2=None, op0=ALU.mult)
+                if on_vector:
+                    nc.vector.tensor_scalar(out=tm[n_load][:, r, cols], in0=m_raw[n_load][:, r, cols],
+                                            scalar1=t_sb[:, r:r + 1], scalar2=None, op0=ALU.mult)
+                else:
+                    nc.scalar.activation(out=tm[n_load][:, r, cols], in_=m_raw[n_load][:, r, cols],
+                                         func=ACT.Copy, scale=t_sb[:, r:r + 1])
 
         def scores(i, h):
+            n_load, qcols = find(q_loads, i)
             for r in range(PACK):
                 if True:
                     rows = slice(h * ROWS, (h + 1) * ROWS)
@@ -125,8 +132,8 @@ def tile_rows_a_tanh_mask_kernel(tc, qT, kT, t, v, mask, out):
                         out=s_ps[h][i % 2][:, r * QT:(r + 1) * QT],
                         lhsT=k_codes[r // 2][rows, cols].bitcast(FP8X4),
                         lhsT_scale=k_scales[r // 2][rows, cols],
-                        rhs=q_codes[i][rows, :].bitcast(FP8X4),
-                        rhs_scale=q_scales[i][rows, :],
+                        rhs=q_codes[n_load][rows, qcols].bitcast(FP8X4),
+                        rhs_scale=q_scales[n_load][rows, qcols],
                         start=True, stop=True)
 
         def tanh(i, h):
@@ -177,7 +184,7 @@ def tile_rows_a_tanh_mask_kernel(tc, qT, kT, t, v, mask, out):
                 in_=y_sb[h][g][:].rearrange("p (x e) -> p x e", e=E))
 
         nc.sync.dma_start(out=k_raw[:], in_=k_hbm)
-        nc.gpsimd.dma_start(out=t_sb[:], in_=t_hbm)
+        nc.scalar.dma_start(out=t_sb[:], in_=t_hbm)
         load_q(0)
         load_q(1)
         load_m(0)
@@ -200,46 +207,45 @@ def tile_rows_a_tanh_mask_kernel(tc, qT, kT, t, v, mask, out):
         scores(0, 0)
         scores(0, 1)
         cast_q(1, False)
+        make_tm(0, True)
         quant_q(1)
-        scores(1, 0)
-        scores(1, 1)
-        make_tm(0)
         tanh(0, 0)
+        scores(1, 0)
         tanh(0, 1)
-        tanh(1, 0)
+        scores(1, 1)
         weigh(0, 0)
-        weigh(0, 1)
         cast_q(2, False)
         cast_q(3, True)
-        quant_w(0, (0, 1))
-        make_tm(1)
-        quant_q(2)
-        quant_q(3)
-        tanh(1, 1)
+        weigh(0, 1)
+        quant_q(2, 2)
+        tanh(1, 0)
         scores(2, 0)
+        make_tm(1, False)
+        quant_w(0, (0, 1))
+        tanh(1, 1)
         scores(2, 1)
-        weigh(1, 0)
-        weigh(1, 1)
-        cast_v(0, False)
+        cast_v(0, True)
         tanh(2, 0)
-        make_tm(2)
-        quant_v(0)
-        quant_w(1, (0, 1))
+        weigh(1, 0)
         scores(3, 0)
+        weigh(1, 1)
+        make_tm(2, False)
+        quant_v(0)
+        cast_v(1, True)
+        quant_w(1, (0, 1))
         tanh(2, 1)
         scores(3, 1)
-        weigh(2, 0)
-        cast_v(1, False)
-        weigh(2, 1)
         product(0, 0)
         product(1, 0)
-        tanh(3, 0)
-        make_tm(3)
+        weigh(2, 0)
         quant_v(1)
-        quant_w(2, (0, 1))
-        tanh(3, 1)
+        weigh(2, 1)
         product(0, 1)
         product(1, 1)
+        tanh(3, 0)
+        make_tm(3, False)
+        quant_w(2, (0, 1))
+        tanh(3, 1)
         product(2, 0)
         product(2, 1)
         finish(0, 0, False, nc.sync)

@@ -63,7 +63,8 @@ def tile_rows_a_tanh_mask_kernel(tc, qT, kT, t, v, mask, out):
         y_sb = [[sbt("y%d_%d" % (h, b), [P, n * E], F32) for b, n in enumerate((2, 1, 1))] for h in range(H)]
 
         s_ps = [[ps.tile([P, PACK * QT], F32, name="s%d_%d" % (h, b)) for b in range(2)] for h in range(H)]
-        y_ps = [[ps.tile([P, PACK * E], F32, name="yp%d_%d" % (h, b)) for b in range(2)] for h in range(H)]
+        y_ps = [ps.tile([P, PACK * E], F32, name="yp%d" % b) for b in range(3)]
+        y_both = sbt("y_both", [P, H * E], F32)
 
         def find(loads, i, count=1):
             for n_load, (a, n) in enumerate(loads):
@@ -148,10 +149,10 @@ def tile_rows_a_tanh_mask_kernel(tc, qT, kT, t, v, mask, out):
                 op=ALU.mult)
 
         def product(i, h):
-            b, x = y_place[i]
+            b, x = (2, h) if i == 2 else (h, min(i, 2))
             cols = slice(h * QT, (h + 1) * QT)
             nc.tensor.matmul_mx(
-                out=y_ps[h][b][:, x * E:(x + 1) * E],
+                out=y_ps[b][:, x * E:(x + 1) * E],
                 lhsT=w_codes[i][:, cols].bitcast(FP8X4),
                 lhsT_scale=w_scales[i][:, cols],
                 rhs=v_codes[h][:].bitcast(FP8X4),
@@ -170,10 +171,15 @@ def tile_rows_a_tanh_mask_kernel(tc, qT, kT, t, v, mask, out):
         def quant_k(a):
             quant(k_codes[a][:], k_scales[a][:], k_bf[a][:])
 
+        def finish_both():
+            nc.scalar.activation(out=y_both[:], in_=y_ps[2][:, :H * E], func=ACT.Copy, scale=1.0 / 16.0)
+            nc.sync.dma_start(out=out[:, 2 * QT:3 * QT, :].rearrange("h p e -> p h e"),
+                              in_=y_both[:].rearrange("p (h e) -> p h e", e=E))
+
         def finish(h, g, on_vector, queue):
             a, n = groups[g]
-            b, x = y_place[a]
-            src = y_ps[h][b][:, x * E:(x + n) * E]
+            x = min(a, 2)
+            src = y_ps[h][:, x * E:(x + n) * E]
             if on_vector:
                 nc.vector.tensor_scalar(out=y_sb[h][g][:], in0=src, scalar1=1.0 / 16.0,
                                         scalar2=None, op0=ALU.mult)
@@ -238,8 +244,8 @@ def tile_rows_a_tanh_mask_kernel(tc, qT, kT, t, v, mask, out):
         product(0, 0)
         product(1, 0)
         weigh(2, 0)
-        quant_v(1)
         weigh(2, 1)
+        quant_v(1)
         product(0, 1)
         product(1, 1)
         tanh(3, 0)
@@ -252,8 +258,7 @@ def tile_rows_a_tanh_mask_kernel(tc, qT, kT, t, v, mask, out):
         weigh(3, 0)
         finish(1, 0, False, nc.sync)
         weigh(3, 1)
-        finish(0, 1, False, nc.sync)
-        finish(1, 1, False, nc.sync)
+        finish_both()
         quant_w(3, (0,))
         quant_w(3, (1,))
         product(3, 0)

from contextlib import ExitStack

import concourse.mybir as mybir

H, D, NQ, N, E = 2, 256, 512, 512, 128
FLOPS = 2 * H * N * NQ * D + 2 * H * NQ * N * E

F32 = mybir.dt.float32
BF16 = mybir.dt.bfloat16
U32 = mybir.dt.uint32
U8 = mybir.dt.uint8
FP8X4 = mybir.dt.float8_e4m3fn_x4
ACT = mybir.ActivationFunctionType
ALU = mybir.AluOpType

P = 128
ROWS = 64
PACK = 4
QT = 128
TILES = NQ // QT


def tile_rows_a_tanh_mask_kernel(tc, qT, kT, t, v, mask, out):
    nc = tc.nc
    with ExitStack() as ctx:
        sb = ctx.enter_context(tc.tile_pool(name="sb", bufs=1))
        ps = ctx.enter_context(tc.psum_pool(name="ps", bufs=1))
        ctx.enter_context(tc.manual_schedule())

        def sbt(name, shape, dtype):
            return sb.tile(shape, dtype, name=name, align_bytes=64)

        q_hbm = qT.rearrange("h (p j) n -> (h p) j n", j=PACK)
        k_hbm = kT.rearrange("h (p j) n -> (h p) j n", j=PACK)
        m_hbm = mask.rearrange("(p r) n -> p r n", r=PACK)
        v_hbm = v.rearrange("h (p j) e -> p h (j e)", j=PACK)
        t_hbm = t.rearrange("(p r) o -> p (r o)", r=PACK)

        q_loads = [(0, 1), (1, 1), (2, 2)]
        m_loads = [(0, 1), (1, 1), (2, 1), (3, 1)]
        q_raw = [sbt("q_raw%d" % i, [P, PACK, n * QT], F32) for i, (a, n) in enumerate(q_loads)]
        m_raw = [sbt("m_raw%d" % i, [P, PACK, n * QT], F32) for i, (a, n) in enumerate(m_loads)]
        tm = [sbt("tm%d" % i, [P, PACK, n * QT], F32) for i, (a, n) in enumerate(m_loads)]
        k_raw = sbt("k_raw", [P, PACK, N], F32)
        v_raw = [sbt("v_raw%d" % h, [P, PACK * E], F32) for h in range(H)]
        t_sb = sbt("t_sb", [P, PACK], F32)
        zero_in = sbt("zero_in", [P, 1], F32)
        zero = sbt("zero", [P, 1], F32)

        q_bf = [sbt("q_bf%d" % i, [P, n * QT * PACK], BF16) for i, (a, n) in enumerate(q_loads)]
        q_codes = [sbt("q_codes%d" % i, [P, n * QT], U32) for i, (a, n) in enumerate(q_loads)]
        q_scales = [sbt("q_scales%d" % i, [P, n * QT], U8) for i, (a, n) in enumerate(q_loads)]
        k_bf = [sbt("k_bf%d" % a, [P, 2 * P * PACK], BF16) for a in range(2)]
        k_codes = [sbt("k_codes%d" % a, [P, 2 * P], U32) for a in range(2)]
        k_scales = [sbt("k_scales%d" % a, [P, 2 * P], U8) for a in range(2)]
        v_bf = [sbt("v_bf%d" % h, [P, E * PACK], BF16) for h in range(H)]
        v_codes = [sbt("v_codes%d" % h, [P, E], U32) for h in range(H)]
        v_scales = [sbt("v_scales%d" % h, [P, E], U8) for h in range(H)]
        p_sb = [[sbt("p%d_%d" % (i, h), [P, PACK * QT], F32) for h in range(H)] for i in range(TILES)]
        w_bf = [sbt("w_bf%d" % i, [P, H * QT * PACK], BF16) for i in range(TILES)]
        w_codes = [sbt("w_codes%d" % i, [P, H * QT], U32) for i in range(TILES)]
        w_scales = [sbt("w_scales%d" % i, [P, H * QT], U8) for i in range(TILES)]
        y_sb = [[sbt("y%d_%d" % (h, b), [P, n * E], F32) for b, n in enumerate((2, 1, 1))] for h in range(H)]

        s_ps = [[ps.tile([P, PACK * QT], F32, name="s%d_%d" % (h, b)) for b in range(2)] for h in range(H)]
        y_ps = [ps.tile([P, PACK * E], F32, name="yp%d" % b) for b in range(3)]
        y_both = sbt("y_both", [P, H * E], F32)

        def find(loads, i, count=1):
            for n_load, (a, n) in enumerate(loads):
                if a <= i < a + n:
                    return n_load, slice((i - a) * QT, (i - a + count) * QT)
            raise ValueError("no load")

        def load_q(n_load):
            a, n = q_loads[n_load]
            nc.sync.dma_start(out=q_raw[n_load][:], in_=q_hbm[:, :, a * QT:(a + n) * QT])

        def load_m(n_load):
            a, n = m_loads[n_load]
            nc.sync.dma_start(out=m_raw[n_load][:], in_=m_hbm[:, :, a * QT:(a + n) * QT])

        def cast(on_vector, dst, src):
            if on_vector:
                nc.vector.tensor_copy(out=dst, in_=src)
            else:
                nc.scalar.copy(out=dst, in_=src)

        def cast_q(i, on_vector, count=1):
            n_load, cols = find(q_loads, i, count)
            cast(on_vector,
                 q_bf[n_load][:, cols.start * PACK:cols.stop * PACK].rearrange("p (c i j) -> p c j i", i=2, j=PACK),
                 q_raw[n_load][:, :, cols].rearrange("p j (c i) -> p c j i", i=2))

        def cast_k(a, on_vector):
            cast(on_vector,
                 k_bf[a][:].rearrange("p (r s j) -> p s j r", r=2, j=PACK),
                 k_raw[:].rearrange("p j (s r) -> p s j r", r=PACK)[:, :, :, 2 * a:2 * a + 2])

        def cast_v(h, on_vector):
            cast(on_vector,
                 v_bf[h][:].rearrange("p (c i j) -> p c j i", i=2, j=PACK),
                 v_raw[h][:].rearrange("p (j c i) -> p c j i", i=2, j=PACK))

        def quant(codes, scales, src):
            nc.vector.quantize_mx(out=codes.bitcast(FP8X4), scales=scales, in_=src)

        def quant_q(i, count=1):
            n_load, cols = find(q_loads, i, count)
            quant(q_codes[n_load][:, cols], q_scales[n_load][:, cols], q_bf[n_load][:, cols.start * PACK:cols.stop * PACK])

        def quant_w(i, heads):
            a, b = heads[0], heads[-1] + 1
            quant(w_codes[i][:, a * QT:b * QT], w_scales[i][:, a * QT:b * QT], w_bf[i][:, a * QT * PACK:b * QT * PACK])

        def make_tm(i, on_vector, count=1):
            n_load, cols = find(m_loads, i, count)
            for r in range(PACK):
                if on_vector:
                    nc.vector.tensor_scalar(out=tm[n_load][:, r, cols], in0=m_raw[n_load][:, r, cols],
                                            scalar1=t_sb[:, r:r + 1], scalar2=None, op0=ALU.mult)
                else:
                    nc.scalar.activation(out=tm[n_load][:, r, cols], in_=m_raw[n_load][:, r, cols],
                                         func=ACT.Copy, scale=t_sb[:, r:r + 1])

        def scores(i, h):
            n_load, qcols = find(q_loads, i)
            for r in range(PACK):
                if True:
                    rows = slice(h * ROWS, (h + 1) * ROWS)
                    cols = slice((r % 2) * P, (r % 2 + 1) * P)
                    nc.tensor.matmul_mx(
                        out=s_ps[h][i % 2][:, r * QT:(r + 1) * QT],
                        lhsT=k_codes[r // 2][rows, cols].bitcast(FP8X4),
                        lhsT_scale=k_scales[r // 2][rows, cols],
                        rhs=q_codes[n_load][rows, qcols].bitcast(FP8X4),
                        rhs_scale=q_scales[n_load][rows, qcols],
                        start=True, stop=True)

        def tanh(i, h):
            nc.scalar.activation(out=p_sb[i][h][:], in_=s_ps[h][i % 2][:], func=ACT.Tanh, bias=zero[:])

        def weigh(i, h):
            n_load, cols = find(m_loads, i)
            nc.vector.tensor_tensor(
                out=w_bf[i][:, h * QT * PACK:(h + 1) * QT * PACK].rearrange("p (c i r) -> p c r i", i=2, r=PACK),
                in0=p_sb[i][h][:].rearrange("p (r c i) -> p c r i", i=2, r=PACK),
                in1=tm[n_load][:, :, cols].rearrange("p r (c i) -> p c r i", i=2),
                op=ALU.mult)

        def product(i, h):
            b, x = (2, h) if i == 2 else (h, min(i, 2))
            cols = slice(h * QT, (h + 1) * QT)
            nc.tensor.matmul_mx(
                out=y_ps[b][:, x * E:(x + 1) * E],
                lhsT=w_codes[i][:, cols].bitcast(FP8X4),
                lhsT_scale=w_scales[i][:, cols],
                rhs=v_codes[h][:].bitcast(FP8X4),
                rhs_scale=v_scales[h][:],
                start=True, stop=True)

        y_place = [(0, 0), (0, 1), (1, 0), (0, 2)]
        groups = [(0, 2), (2, 1), (3, 1)]

        def load_v(h):
            nc.sync.dma_start(out=v_raw[h][:], in_=v_hbm[:, h, :])

        def quant_v(h):
            quant(v_codes[h][:], v_scales[h][:], v_bf[h][:])

        def quant_k(a):
            quant(k_codes[a][:], k_scales[a][:], k_bf[a][:])

        def finish_both():
            nc.scalar.activation(out=y_both[:], in_=y_ps[2][:, :H * E], func=ACT.Copy, scale=1.0 / 16.0)
            nc.sync.dma_start(out=out[:, 2 * QT:3 * QT, :].rearrange("h p e -> p h e"),
                              in_=y_both[:].rearrange("p (h e) -> p h e", e=E))

        def finish(h, g, on_vector, queue):
            a, n = groups[g]
            x = min(a, 2)
            src = y_ps[h][:, x * E:(x + n) * E]
            if on_vector:
                nc.vector.tensor_scalar(out=y_sb[h][g][:], in0=src, scalar1=1.0 / 16.0,
                                        scalar2=None, op0=ALU.mult)
            else:
                nc.scalar.activation(out=y_sb[h][g][:], in_=src, func=ACT.Copy, scale=1.0 / 16.0)
            queue.dma_start(
                out=out[h, a * QT:(a + n) * QT, :].rearrange("(x p) e -> p x e", p=QT),
                in_=y_sb[h][g][:].rearrange("p (x e) -> p x e", e=E))

        nc.sync.dma_start(out=k_raw[:], in_=k_hbm)
        nc.scalar.dma_start(out=t_sb[:], in_=t_hbm)
        load_q(0)
        load_q(1)
        load_m(0)
        load_q(2)
        load_m(1)
        load_v(0)
        load_m(2)
        load_v(1)
        load_m(3)

        nc.vector.memset(zero_in[:], 0.0)
        nc.scalar.activation(out=zero[:], in_=zero_in[:], func=ACT.Tanh)

        cast_k(0, True)
        cast_k(1, False)
        cast_q(0, True)
        quant_k(0)
        quant_q(0)
        quant_k(1)
        scores(0, 0)
        scores(0, 1)
        cast_q(1, False)
        make_tm(0, True)
        quant_q(1)
        tanh(0, 0)
        scores(1, 0)
        tanh(0, 1)
        scores(1, 1)
        weigh(0, 0)
        cast_q(2, False)
        cast_q(3, True)
        weigh(0, 1)
        quant_q(2, 2)
        tanh(1, 0)
        scores(2, 0)
        make_tm(1, False)
        quant_w(0, (0, 1))
        tanh(1, 1)
        scores(2, 1)
        cast_v(0, True)
        tanh(2, 0)
        weigh(1, 0)
        scores(3, 0)
        weigh(1, 1)
        make_tm(2, False)
        quant_v(0)
        cast_v(1, True)
        quant_w(1, (0, 1))
        tanh(2, 1)
        scores(3, 1)
        product(0, 0)
        product(1, 0)
        weigh(2, 0)
        weigh(2, 1)
        quant_v(1)
        product(0, 1)
        product(1, 1)
        tanh(3, 0)
        make_tm(3, False)
        quant_w(2, (0, 1))
        tanh(3, 1)
        product(2, 0)
        product(2, 1)
        finish(0, 0, False, nc.sync)
        weigh(3, 0)
        finish(1, 0, False, nc.sync)
        weigh(3, 1)
        finish_both()
        quant_w(3, (0,))
        quant_w(3, (1,))
        product(3, 0)
        product(3, 1)
        finish(0, 2, True, nc.sync)
        finish(1, 2, False, nc.scalar)
